import numpy as np
import ml_dtypes


def mxq(x, axis, fmt="e4m3"):
    dtype, down = {"e4m3": (ml_dtypes.float8_e4m3fn, 7), "e5m2": (ml_dtypes.float8_e5m2, 14)}[fmt]
    v = np.moveaxis(np.asarray(x, np.float32).astype(ml_dtypes.bfloat16).astype(np.float64), axis, -1)
    blocks = v.reshape(v.shape[:-1] + (-1, 32))
    amax = np.abs(blocks).max(-1, keepdims=True)
    byte = np.maximum(np.where(amax > 0, np.frexp(amax)[1] - 1 + 127, 0) - down, 1)
    scale = np.exp2(byte - 127.0)
    codes = (blocks / scale).astype(np.float32).astype(dtype).astype(np.float64)
    return np.moveaxis((codes * scale).reshape(v.shape), -1, axis)


WIDE = False


def mx_kscale(k):
    if not WIDE:
        return np.ones(k)
    levels = np.array([10, -10, 5, -5, 0])
    if k % 512:
        return np.exp2(np.random.permutation(np.resize(levels, k // 32))).repeat(32)
    a = np.empty((k // 512, 16))
    for p in range(k // 512):
        a[p, :8] = np.random.permutation(np.resize(levels, 8))
        for g in range(8):
            far = levels[np.abs(levels - a[p, g]) >= 10]
            a[p, g + 8] = far[np.random.randint(len(far))]
    return np.exp2(a.ravel()).repeat(32)


def f64(x):
    return np.asarray(x).astype(np.float64)


def striped(idx):
    return np.tile(np.asarray(idx).reshape(-1, 16).T, (8, 1)).astype(np.uint16)


def unstriped(offs):
    return offs[:16].T.reshape(-1).astype(np.int64)


E2M1 = np.array([0.0, 0.5, 1.0, 1.5, 2.0, 3.0, 4.0, 6.0, -0.0, -0.5, -1.0, -1.5, -2.0, -3.0, -4.0, -6.0])


def pack_weight(w, fmt):
    k, n = w.shape
    w = f64(np.asarray(w, np.float32).astype(ml_dtypes.bfloat16)).reshape(k // 32, 32, n)
    amax = np.abs(w).max(1)
    if fmt == "e4m3":
        byte = np.frexp(amax)[1] - 1 + 127 - 7
    else:
        mant, ex = np.frexp(amax / 6.0)
        byte = np.where(mant > 0.5, ex, ex - 1) + 127
    byte = np.clip(np.where(amax > 0, byte, 1), 1, 254)
    scaled = (w * np.exp2(127.0 - byte)[:, None, :]).reshape(k, n).astype(np.float32)
    by_word = np.ascontiguousarray(scaled.reshape(k // 512, 128, 4, n).transpose(0, 1, 3, 2))
    if fmt == "e4m3":
        words = by_word.astype(ml_dtypes.float8_e4m3fn).view(np.uint8)
    else:
        c = by_word.astype(ml_dtypes.float4_e2m1fn).view(np.uint8) & 0xF
        words = (c[..., 0::2] | (c[..., 1::2] << 4)).reshape(k // 512, 128, 2 * n)
    return np.ascontiguousarray(words), np.ascontiguousarray(byte.astype(np.uint8).reshape(k // 512, 16, n))


def unpack_weight(words, scales, fmt):
    g, _, n = scales.shape
    words = np.ascontiguousarray(words).reshape(g, 128, n, -1)
    if fmt == "e4m3":
        vals = words.view(ml_dtypes.float8_e4m3fn).astype(np.float64)
    else:
        nib = np.empty((g, 128, n, 4), np.uint8)
        nib[..., 0::2] = words & 0xF
        nib[..., 1::2] = words >> 4
        vals = E2M1[nib]
    vals = vals * np.repeat(np.exp2(scales.astype(np.float64) - 127.0), 8, axis=1)[..., None]
    return vals.transpose(0, 1, 3, 2).reshape(g * 512, n)


B, N, T, D, NQ = 1, 512, 2048, 1024, 128


def setup_inputs():
    n = np.random.standard_normal
    idx = np.random.permutation(T)[:B * N]
    s = mx_kscale(D)[:, None]
    kp = pack_weight(n((D, T)) / s, "e2m1")
    cp = pack_weight(n((D, T)) / s / 12, "e4m3")
    return {
        "qT": (n((B, D, NQ)) * s * (1.00 / np.sqrt(D))).astype(np.float32),
        "k_words": np.ascontiguousarray(kp[0].reshape(1, 2, 128, T, 2).transpose(0, 2, 3, 1, 4)).reshape(1, 128, T, 4),
        "k_scales": kp[1],
        "c_words": cp[0],
        "c_scales": cp[1],
        "offs": striped(idx),
    }


def reference(qT, k_words, k_scales, c_words, c_scales, offs):
    idx = unstriped(offs)
    pick = lambda x, which: x[:, which].reshape(x.shape[0], B, -1).transpose(1, 0, 2)
    k = unpack_weight(k_words.reshape(1, 128, T, 2, 2).transpose(0, 3, 1, 2, 4).reshape(2, 128, 2 * T), k_scales, "e2m1")
    kg = pick(k, idx)
    c = unpack_weight(c_words, c_scales, "e4m3")
    cg = pick(c, idx)
    qq = mxq(f64(qT), 1, "e4m3")
    a = (qq.transpose(0, 2, 1) @ kg) + (qq.transpose(0, 2, 1) @ cg)
    m = np.max(a, axis=-1, keepdims=True)
    e = np.exp(a - m)
    l = np.sum(e, axis=-1, keepdims=True)
    y = e / l
    return y

@@ -1,0 +1,144 @@
+from contextlib import ExitStack
+
+import concourse.mybir as mybir
+
+N, T, D, NQ = 512, 2048, 1024, 128
+FLOPS = 2 * 2 * NQ * N * D
+
+F32 = mybir.dt.float32
+BF16 = mybir.dt.bfloat16
+I32 = mybir.dt.int32
+U32 = mybir.dt.uint32
+U16 = mybir.dt.uint16
+U8 = mybir.dt.uint8
+FP8X4 = mybir.dt.float8_e4m3fn_x4
+FP4X4 = mybir.dt.float4_e2m1fn_x4
+ALU = mybir.AluOpType
+ACT = mybir.ActivationFunctionType
+
+P = 128
+PACK = 4
+PASSES = D // (P * PACK)
+HALF = N // 2
+QUART = 128
+C_ROW = 4
+
+
+def tile_attend_residw_topk_kernel(tc, qT, k_words, k_scales, c_words, c_scales, offs, out):
+    nc = tc.nc
+    with ExitStack() as ctx:
+        held = ctx.enter_context(tc.tile_pool(name="held", bufs=1))
+        psum = ctx.enter_context(tc.psum_pool(name="psum", bufs=1))
+
+        offsets = held.tile([P, N // 16], U16, name="offsets")
+        nc.sync.dma_start(offsets[:], offs)
+
+        ks_all = held.tile([P, PASSES, T // 4], I32, name="ks_all", align_bytes=64)
+        cs_all = held.tile([P, T // 4], I32, name="cs_all", align_bytes=64)
+        warm = held.tile([P, 8], F32, name="warm")
+        nc.vector.memset(ks_all[:], 0)
+        nc.vector.memset(cs_all[:], 0)
+        nc.vector.memset(warm[:], 0.0)
+
+        ks_hbm = k_scales.bitcast(I32)
+        for r, queue in enumerate((nc.sync, nc.scalar, nc.scalar, nc.gpsimd)):
+            queue.dma_start(ks_all[r:P:32, :, :], ks_hbm[:, r:16:4, :].rearrange("o q t -> q o t"))
+        cs_hbm = c_scales.bitcast(I32)
+        for quad in range(4):
+            row = 32 * quad + C_ROW
+            nc.gpsimd.dma_start(cs_all[row : row + 8, :], cs_hbm[:, 4 * quad : 4 * quad + 4, :])
+
+        q_raw = [held.tile([P, PACK * NQ], F32, name=f"q_raw{o}") for o in range(PASSES)]
+        q_hbm = qT[0].rearrange("(o p j) w -> o p (j w)", o=PASSES, j=PACK)
+        nc.sync.dma_start(q_raw[0][:], q_hbm[0])
+        kw_all = held.tile([P, T], I32, name="kw_all", align_bytes=64)
+        nc.sync.dma_start(kw_all[:], k_words[0].rearrange("p t b -> p (t b)").bitcast(I32))
+        nc.sync.dma_start(q_raw[1][:], q_hbm[1])
+        cw_all = [held.tile([P, T], I32, name=f"cw_all{o}", align_bytes=64) for o in range(PASSES)]
+        for o in range(PASSES):
+            nc.sync.dma_start(cw_all[o][:], c_words[o].rearrange("p t b -> p (t b)").bitcast(I32))
+
+        warm_out = held.tile([P, 8], F32, name="warm_out")
+        nc.scalar.activation(warm_out[:], warm[:], ACT.Exp)
+
+        q_bf = held.tile([P, PASSES, NQ, PACK], BF16, name="q_bf", align_bytes=64)
+        for o in range(PASSES):
+            nc.scalar.copy(q_bf[:, o, :, :], q_raw[o][:].rearrange("p (j w) -> p w j", j=PACK))
+
+        ks_got = held.tile([P, PASSES, N], U8, name="ks_got", align_bytes=64)
+        for o in range(PASSES):
+            nc.vector.tensor_copy(ks_got[:, o, :], ks_all[:, o, :].bitcast(U8).indirect(offsets[:]))
+
+        q_codes = held.tile([P, PASSES * NQ], U32, name="q_codes", align_bytes=64)
+        q_scales = held.tile([P, PASSES * NQ], U8, name="q_scales", align_bytes=64)
+        nc.vector.quantize_mx(
+            out=q_codes[:].bitcast(FP8X4), scales=q_scales[:], in_=q_bf[:].rearrange("p o w j -> p (o w j)")
+        )
+
+        kw_got = held.tile([P, N], U32, name="kw_got", align_bytes=64)
+        nc.vector.tensor_copy(kw_got[:], kw_all[:].bitcast(U32).indirect(offsets[:]))
+        kw_pass = held.tile([P, PASSES, N], U16, name="kw_pass", align_bytes=64)
+        kw_pairs = kw_got[:].bitcast(U16).rearrange("p (n o) -> p o n", o=PASSES)
+        for o in range(PASSES):
+            nc.vector.tensor_copy(kw_pass[:, o, :], kw_pairs[:, o, :])
+
+        cs_got = held.tile([P, N], U8, name="cs_got", align_bytes=64)
+        nc.vector.tensor_copy(cs_got[:], cs_all[:].bitcast(U8).indirect(offsets[:]))
+
+        cw_got = [held.tile([P, N], U32, name=f"cw_got{o}", align_bytes=64) for o in range(PASSES)]
+        nc.vector.tensor_copy(cw_got[0][:], cw_all[0][:].bitcast(U32).indirect(offsets[:]))
+        for h in range(2):
+            nc.vector.tensor_copy(
+                cw_got[1][:, h * HALF : (h + 1) * HALF],
+                cw_all[1][:].bitcast(U32).indirect(offsets[:, h * HALF // 16 : (h + 1) * HALF // 16]),
+            )
+
+        banks = [psum.tile([P, HALF], F32, name=f"bank{h}") for h in range(2)]
+
+        def q_operand(o):
+            cols = slice(o * NQ, (o + 1) * NQ)
+            return q_codes[:, cols].bitcast(FP8X4), q_scales[:, cols]
+
+        for o in range(PASSES):
+            lhsT, lhsT_scale = q_operand(o)
+            for n0 in range(0, N, QUART):
+                h, c0 = divmod(n0, HALF)
+                nc.tensor.matmul_mx(
+                    out=banks[h][:, c0 : c0 + QUART],
+                    lhsT=lhsT,
+                    lhsT_scale=lhsT_scale,
+                    rhs=kw_pass[:, o, n0 : n0 + QUART].bitcast(FP4X4),
+                    rhs_scale=ks_got[:, o, n0 : n0 + QUART],
+                    start=(o == 0 and c0 == 0),
+                    stop=False,
+                )
+        for o in range(PASSES):
+            lhsT, lhsT_scale = q_operand(o)
+            for h in range(2):
+                cols = slice(h * HALF, (h + 1) * HALF)
+                nc.tensor.matmul_mx(
+                    out=banks[h][:],
+                    lhsT=lhsT,
+                    lhsT_scale=lhsT_scale,
+                    rhs=cw_got[o][:, cols].bitcast(FP8X4),
+                    rhs_scale=cs_got[C_ROW + 4 * o : P, cols],
+                    start=False,
+                    stop=(o == PASSES - 1),
+                )
+
+        neg = held.tile([P, N], F32, name="neg")
+        neg_max = [held.tile([P, 1], F32, name=f"neg_max{h}") for h in range(2)]
+        nc.vector.tensor_scalar(neg[:, 0:HALF], banks[0][:], -1.0, None, ALU.mult, ALU.min, accum_out=neg_max[0][:])
+        nc.vector.tensor_scalar(
+            neg[:, HALF:N], banks[1][:], -1.0, neg_max[0][:], ALU.mult, ALU.min, accum_out=neg_max[1][:]
+        )
+        e = held.tile([P, N], F32, name="e")
+        total = held.tile([P, 1], F32, name="total")
+        nc.scalar.activation(e[:], neg[:], ACT.Exp, bias=neg_max[1][:], scale=-1.0, accum_out=total[:])
+        inv = held.tile([P, 1], F32, name="inv")
+        nc.vector.reciprocal(inv[:], total[:])
+        y = held.tile([P, N], F32, name="y")
+        for h, queue in enumerate((nc.sync, nc.scalar)):
+            cols = slice(h * HALF, (h + 1) * HALF)
+            nc.vector.tensor_scalar(y[:, cols], e[:, cols], inv[:], None, ALU.mult)
+            queue.dma_start(out[0][:, cols], y[:, cols])

@@ -33,41 +33,51 @@ def tile_attend_residw_topk_kernel(tc, qT, k_words, k_scales, c_words, c_scales,
         offsets = held.tile([P, N // 16], U16, name="offsets")
         nc.sync.dma_start(offsets[:], offs)
 
-        ks_all = held.tile([P, PASSES, T // 4], I32, name="ks_all", align_bytes=64)
+        ks_all = held.tile([P, T // 4], I32, name="ks_all", align_bytes=64)
         cs_all = held.tile([P, T // 4], I32, name="cs_all", align_bytes=64)
+        ks_moved = held.tile([P, N // 4], I32, name="ks_moved", align_bytes=64)
+        cs_moved = held.tile([P, N // 4], I32, name="cs_moved", align_bytes=64)
         warm = held.tile([P, 8], F32, name="warm")
         nc.vector.memset(ks_all[:], 0)
         nc.vector.memset(cs_all[:], 0)
         nc.vector.memset(warm[:], 0.0)
+        nc.vector.memset(ks_moved[:], 0)
+        nc.vector.memset(cs_moved[:], 0)
 
-        ks_hbm = k_scales.bitcast(I32)
-        for r, queue in enumerate((nc.sync, nc.scalar, nc.scalar, nc.gpsimd)):
-            queue.dma_start(ks_all[r:P:32, :, :], ks_hbm[:, r:16:4, :].rearrange("o q t -> q o t"))
-        cs_hbm = c_scales.bitcast(I32)
-        for quad in range(4):
-            row = 32 * quad + C_ROW
-            nc.gpsimd.dma_start(cs_all[row : row + 8, :], cs_hbm[:, 4 * quad : 4 * quad + 4, :])
+        def load_scales(tile, scales, first_row):
+            rows = scales.bitcast(I32)
+            for r in range(4):
+                nc.sync.dma_start(tile[first_row + r : P : 16, :], rows[:, r:16:4, :].rearrange("o q t -> q o t"))
 
-        q_raw = [held.tile([P, PACK * NQ], F32, name=f"q_raw{o}") for o in range(PASSES)]
-        q_hbm = qT[0].rearrange("(o p j) w -> o p (j w)", o=PASSES, j=PACK)
-        nc.sync.dma_start(q_raw[0][:], q_hbm[0])
+        q_raw = held.tile([P, PASSES, PACK * NQ], F32, name="q_raw")
         kw_all = held.tile([P, T], I32, name="kw_all", align_bytes=64)
-        nc.sync.dma_start(kw_all[:], k_words[0].rearrange("p t b -> p (t b)").bitcast(I32))
-        nc.sync.dma_start(q_raw[1][:], q_hbm[1])
         cw_all = [held.tile([P, T], I32, name=f"cw_all{o}", align_bytes=64) for o in range(PASSES)]
-        for o in range(PASSES):
-            nc.sync.dma_start(cw_all[o][:], c_words[o].rearrange("p t b -> p (t b)").bitcast(I32))
+        nc.sync.dma_start(q_raw[:], qT[0].rearrange("(o p j) w -> p o (j w)", o=PASSES, j=PACK))
+        load_scales(ks_all, k_scales, 0)
+        nc.sync.dma_start(cw_all[0][:], c_words[0].rearrange("p t b -> p (t b)").bitcast(I32))
+        load_scales(cs_all, c_scales, C_ROW)
+        nc.sync.dma_start(kw_all[:], k_words[0].rearrange("p t b -> p (t b)").bitcast(I32))
+        nc.sync.dma_start(cw_all[1][:], c_words[1].rearrange("p t b -> p (t b)").bitcast(I32))
 
         warm_out = held.tile([P, 8], F32, name="warm_out")
         nc.scalar.activation(warm_out[:], warm[:], ACT.Exp)
 
         q_bf = held.tile([P, PASSES, NQ, PACK], BF16, name="q_bf", align_bytes=64)
         for o in range(PASSES):
-            nc.scalar.copy(q_bf[:, o, :, :], q_raw[o][:].rearrange("p (j w) -> p w j", j=PACK))
+            nc.scalar.copy(q_bf[:, o, :, :], q_raw[:, o, :].rearrange("p (j w) -> p w j", j=PACK))
 
-        ks_got = held.tile([P, PASSES, N], U8, name="ks_got", align_bytes=64)
-        for o in range(PASSES):
-            nc.vector.tensor_copy(ks_got[:, o, :], ks_all[:, o, :].bitcast(U8).indirect(offsets[:]))
+        ks_got = held.tile([P, N], U8, name="ks_got", align_bytes=64)
+        nc.vector.tensor_copy(ks_got[:], ks_all[:].bitcast(U8).indirect(offsets[:]))
+        nc.scalar.dma_start(ks_moved[0 : P - 16, :], ks_got[:].bitcast(I32)[16:P, :])
+        ks_plane = [ks_got[:], ks_moved[:].bitcast(U8)]
+
+        cw_got = [held.tile([P, N], U32, name=f"cw_got{o}", align_bytes=64) for o in range(PASSES)]
+        nc.vector.tensor_copy(cw_got[0][:], cw_all[0][:].bitcast(U32).indirect(offsets[:]))
+
+        cs_got = held.tile([P, N], U8, name="cs_got", align_bytes=64)
+        nc.vector.tensor_copy(cs_got[:], cs_all[:].bitcast(U8).indirect(offsets[:]))
+        nc.scalar.dma_start(cs_moved[0 : P - 16, :], cs_got[:].bitcast(I32)[16:P, :])
+        cs_plane = [cs_got[:], cs_moved[:].bitcast(U8)]
 
         q_codes = held.tile([P, PASSES * NQ], U32, name="q_codes", align_bytes=64)
         q_scales = held.tile([P, PASSES * NQ], U8, name="q_scales", align_bytes=64)
@@ -82,11 +92,6 @@ def tile_attend_residw_topk_kernel(tc, qT, k_words, k_scales, c_words, c_scales,
         for o in range(PASSES):
             nc.vector.tensor_copy(kw_pass[:, o, :], kw_pairs[:, o, :])
 
-        cs_got = held.tile([P, N], U8, name="cs_got", align_bytes=64)
-        nc.vector.tensor_copy(cs_got[:], cs_all[:].bitcast(U8).indirect(offsets[:]))
-
-        cw_got = [held.tile([P, N], U32, name=f"cw_got{o}", align_bytes=64) for o in range(PASSES)]
-        nc.vector.tensor_copy(cw_got[0][:], cw_all[0][:].bitcast(U32).indirect(offsets[:]))
         for h in range(2):
             nc.vector.tensor_copy(
                 cw_got[1][:, h * HALF : (h + 1) * HALF],
@@ -99,6 +104,21 @@ def tile_attend_residw_topk_kernel(tc, qT, k_words, k_scales, c_words, c_scales,
             cols = slice(o * NQ, (o + 1) * NQ)
             return q_codes[:, cols].bitcast(FP8X4), q_scales[:, cols]
 
+        def fine_pass(o):
+            lhsT, lhsT_scale = q_operand(o)
+            for h in range(2):
+                cols = slice(h * HALF, (h + 1) * HALF)
+                nc.tensor.matmul_mx(
+                    out=banks[h][:],
+                    lhsT=lhsT,
+                    lhsT_scale=lhsT_scale,
+                    rhs=cw_got[o][:, cols].bitcast(FP8X4),
+                    rhs_scale=cs_plane[o][C_ROW:P, cols],
+                    start=(o == 0),
+                    stop=(o == PASSES - 1),
+                )
+
+        fine_pass(0)
         for o in range(PASSES):
             lhsT, lhsT_scale = q_operand(o)
             for n0 in range(0, N, QUART):
@@ -108,23 +128,11 @@ def tile_attend_residw_topk_kernel(tc, qT, k_words, k_scales, c_words, c_scales,
                     lhsT=lhsT,
                     lhsT_scale=lhsT_scale,
                     rhs=kw_pass[:, o, n0 : n0 + QUART].bitcast(FP4X4),
-                    rhs_scale=ks_got[:, o, n0 : n0 + QUART],
-                    start=(o == 0 and c0 == 0),
+                    rhs_scale=ks_plane[o][:, n0 : n0 + QUART],
+                    start=False,
                     stop=False,
                 )
-        for o in range(PASSES):
-            lhsT, lhsT_scale = q_operand(o)
-            for h in range(2):
-                cols = slice(h * HALF, (h + 1) * HALF)
-                nc.tensor.matmul_mx(
-                    out=banks[h][:],
-                    lhsT=lhsT,
-                    lhsT_scale=lhsT_scale,
-                    rhs=cw_got[o][:, cols].bitcast(FP8X4),
-                    rhs_scale=cs_got[C_ROW + 4 * o : P, cols],
-                    start=False,
-                    stop=(o == PASSES - 1),
-                )
+        fine_pass(1)
 
         neg = held.tile([P, N], F32, name="neg")
         neg_max = [held.tile([P, 1], F32, name=f"neg_max{h}") for h in range(2)]

@@ -31,9 +31,7 @@ def tile_attend_residw_topk_kernel(tc, qT, k_words, k_scales, c_words, c_scales,
         psum = ctx.enter_context(tc.psum_pool(name="psum", bufs=1))
 
         offsets = held.tile([P, N // 16], U16, name="offsets")
-        nc.sync.dma_start(offsets[:], offs)
-
-        ks_all = held.tile([P, T // 4], I32, name="ks_all", align_bytes=64)
+        ks_all = held.tile([P, T // 4], I32, name="ks_all", tag="ks_then_q", align_bytes=64)
         cs_all = held.tile([P, T // 4], I32, name="cs_all", align_bytes=64)
         ks_moved = held.tile([P, N // 4], I32, name="ks_moved", align_bytes=64)
         cs_moved = held.tile([P, N // 4], I32, name="cs_moved", align_bytes=64)
@@ -54,6 +52,7 @@ def tile_attend_residw_topk_kernel(tc, qT, k_words, k_scales, c_words, c_scales,
         cw_all = [held.tile([P, T], I32, name=f"cw_all{o}", align_bytes=64) for o in range(PASSES)]
         nc.sync.dma_start(q_raw[:], qT[0].rearrange("(o p j) w -> p o (j w)", o=PASSES, j=PACK))
         load_scales(ks_all, k_scales, 0)
+        nc.sync.dma_start(offsets[:], offs)
         nc.sync.dma_start(cw_all[0][:], c_words[0].rearrange("p t b -> p (t b)").bitcast(I32))
         load_scales(cs_all, c_scales, C_ROW)
         nc.sync.dma_start(kw_all[:], k_words[0].rearrange("p t b -> p (t b)").bitcast(I32))
@@ -79,7 +78,7 @@ def tile_attend_residw_topk_kernel(tc, qT, k_words, k_scales, c_words, c_scales,
         nc.scalar.dma_start(cs_moved[0 : P - 16, :], cs_got[:].bitcast(I32)[16:P, :])
         cs_plane = [cs_got[:], cs_moved[:].bitcast(U8)]
 
-        q_codes = held.tile([P, PASSES * NQ], U32, name="q_codes", align_bytes=64)
+        q_codes = held.tile([P, PASSES * NQ], U32, name="q_codes", tag="ks_then_q", align_bytes=64)
         q_scales = held.tile([P, PASSES * NQ], U8, name="q_scales", align_bytes=64)
         nc.vector.quantize_mx(
             out=q_codes[:].bitcast(FP8X4), scales=q_scales[:], in_=q_bf[:].rearrange("p o w j -> p (o w j)")

@@ -31,32 +31,36 @@ def tile_attend_residw_topk_kernel(tc, qT, k_words, k_scales, c_words, c_scales,
         psum = ctx.enter_context(tc.psum_pool(name="psum", bufs=1))
 
         offsets = held.tile([P, N // 16], U16, name="offsets")
-        ks_all = held.tile([P, T // 4], I32, name="ks_all", tag="ks_then_q", align_bytes=64)
-        cs_all = held.tile([P, T // 4], I32, name="cs_all", align_bytes=64)
-        ks_moved = held.tile([P, N // 4], I32, name="ks_moved", align_bytes=64)
-        cs_moved = held.tile([P, N // 4], I32, name="cs_moved", align_bytes=64)
+        ks_all = held.tile([P, T // 4], I32, name="ks_all", align_bytes=64)
+        cs_all = held.tile([P, T // 4], I32, name="cs_all", tag="cs_then_q", align_bytes=64)
+        ks_planes = held.tile([P, PASSES, N // 4], I32, name="ks_planes", align_bytes=64)
+        cs_planes = held.tile([P, PASSES, N // 4], I32, name="cs_planes", align_bytes=64)
         warm = held.tile([P, 8], F32, name="warm")
         nc.vector.memset(ks_all[:], 0)
         nc.vector.memset(cs_all[:], 0)
         nc.vector.memset(warm[:], 0.0)
-        nc.vector.memset(ks_moved[:], 0)
-        nc.vector.memset(cs_moved[:], 0)
+        nc.vector.memset(ks_planes[:], 0)
+        nc.vector.memset(cs_planes[:], 0)
 
-        def load_scales(tile, scales, first_row):
-            rows = scales.bitcast(I32)
-            for r in range(4):
-                nc.sync.dma_start(tile[first_row + r : P : 16, :], rows[:, r:16:4, :].rearrange("o q t -> q o t"))
+        def load_scales(tile, scales):
+            nc.sync.dma_start(tile[0:P:4, :], scales.bitcast(I32).rearrange("o f t -> f o t"))
+
+        def move_scales(planes, got, first_row):
+            for quad in range(0, P, 32):
+                nc.scalar.dma_start(
+                    planes[quad + first_row : quad + first_row + 4, :, :], got[:].bitcast(I32)[quad : quad + 32 : 4, :]
+                )
 
         q_raw = held.tile([P, PASSES, PACK * NQ], F32, name="q_raw")
         kw_all = held.tile([P, T], I32, name="kw_all", align_bytes=64)
         cw_all = [held.tile([P, T], I32, name=f"cw_all{o}", align_bytes=64) for o in range(PASSES)]
         nc.sync.dma_start(q_raw[:], qT[0].rearrange("(o p j) w -> p o (j w)", o=PASSES, j=PACK))
-        load_scales(ks_all, k_scales, 0)
         nc.sync.dma_start(offsets[:], offs)
-        nc.sync.dma_start(cw_all[0][:], c_words[0].rearrange("p t b -> p (t b)").bitcast(I32))
-        load_scales(cs_all, c_scales, C_ROW)
+        load_scales(ks_all, k_scales)
+        load_scales(cs_all, c_scales)
         nc.sync.dma_start(kw_all[:], k_words[0].rearrange("p t b -> p (t b)").bitcast(I32))
-        nc.sync.dma_start(cw_all[1][:], c_words[1].rearrange("p t b -> p (t b)").bitcast(I32))
+        for o in range(PASSES):
+            nc.sync.dma_start(cw_all[o][:], c_words[o].rearrange("p t b -> p (t b)").bitcast(I32))
 
         warm_out = held.tile([P, 8], F32, name="warm_out")
         nc.scalar.activation(warm_out[:], warm[:], ACT.Exp)
@@ -67,18 +71,13 @@ def tile_attend_residw_topk_kernel(tc, qT, k_words, k_scales, c_words, c_scales,
 
         ks_got = held.tile([P, N], U8, name="ks_got", align_bytes=64)
         nc.vector.tensor_copy(ks_got[:], ks_all[:].bitcast(U8).indirect(offsets[:]))
-        nc.scalar.dma_start(ks_moved[0 : P - 16, :], ks_got[:].bitcast(I32)[16:P, :])
-        ks_plane = [ks_got[:], ks_moved[:].bitcast(U8)]
-
-        cw_got = [held.tile([P, N], U32, name=f"cw_got{o}", align_bytes=64) for o in range(PASSES)]
-        nc.vector.tensor_copy(cw_got[0][:], cw_all[0][:].bitcast(U32).indirect(offsets[:]))
+        move_scales(ks_planes, ks_got, 0)
 
         cs_got = held.tile([P, N], U8, name="cs_got", align_bytes=64)
         nc.vector.tensor_copy(cs_got[:], cs_all[:].bitcast(U8).indirect(offsets[:]))
-        nc.scalar.dma_start(cs_moved[0 : P - 16, :], cs_got[:].bitcast(I32)[16:P, :])
-        cs_plane = [cs_got[:], cs_moved[:].bitcast(U8)]
+        move_scales(cs_planes, cs_got, C_ROW)
 
-        q_codes = held.tile([P, PASSES * NQ], U32, name="q_codes", tag="ks_then_q", align_bytes=64)
+        q_codes = held.tile([P, PASSES * NQ], U32, name="q_codes", tag="cs_then_q", align_bytes=64)
         q_scales = held.tile([P, PASSES * NQ], U8, name="q_scales", align_bytes=64)
         nc.vector.quantize_mx(
             out=q_codes[:].bitcast(FP8X4), scales=q_scales[:], in_=q_bf[:].rearrange("p o w j -> p (o w j)")
@@ -91,6 +90,8 @@ def tile_attend_residw_topk_kernel(tc, qT, k_words, k_scales, c_words, c_scales,
         for o in range(PASSES):
             nc.vector.tensor_copy(kw_pass[:, o, :], kw_pairs[:, o, :])
 
+        cw_got = [held.tile([P, N], U32, name=f"cw_got{o}", align_bytes=64) for o in range(PASSES)]
+        nc.vector.tensor_copy(cw_got[0][:], cw_all[0][:].bitcast(U32).indirect(offsets[:]))
         for h in range(2):
             nc.vector.tensor_copy(
                 cw_got[1][:, h * HALF : (h + 1) * HALF],
@@ -103,21 +104,6 @@ def tile_attend_residw_topk_kernel(tc, qT, k_words, k_scales, c_words, c_scales,
             cols = slice(o * NQ, (o + 1) * NQ)
             return q_codes[:, cols].bitcast(FP8X4), q_scales[:, cols]
 
-        def fine_pass(o):
-            lhsT, lhsT_scale = q_operand(o)
-            for h in range(2):
-                cols = slice(h * HALF, (h + 1) * HALF)
-                nc.tensor.matmul_mx(
-                    out=banks[h][:],
-                    lhsT=lhsT,
-                    lhsT_scale=lhsT_scale,
-                    rhs=cw_got[o][:, cols].bitcast(FP8X4),
-                    rhs_scale=cs_plane[o][C_ROW:P, cols],
-                    start=(o == 0),
-                    stop=(o == PASSES - 1),
-                )
-
-        fine_pass(0)
         for o in range(PASSES):
             lhsT, lhsT_scale = q_operand(o)
             for n0 in range(0, N, QUART):
@@ -127,11 +113,23 @@ def tile_attend_residw_topk_kernel(tc, qT, k_words, k_scales, c_words, c_scales,
                     lhsT=lhsT,
                     lhsT_scale=lhsT_scale,
                     rhs=kw_pass[:, o, n0 : n0 + QUART].bitcast(FP4X4),
-                    rhs_scale=ks_plane[o][:, n0 : n0 + QUART],
-                    start=False,
+                    rhs_scale=ks_planes[:, o, :].bitcast(U8)[:, n0 : n0 + QUART],
+                    start=(o == 0 and c0 == 0),
                     stop=False,
                 )
-        fine_pass(1)
+        for o in range(PASSES):
+            lhsT, lhsT_scale = q_operand(o)
+            for h in range(2):
+                cols = slice(h * HALF, (h + 1) * HALF)
+                nc.tensor.matmul_mx(
+                    out=banks[h][:],
+                    lhsT=lhsT,
+                    lhsT_scale=lhsT_scale,
+                    rhs=cw_got[o][:, cols].bitcast(FP8X4),
+                    rhs_scale=cs_planes[C_ROW:P, o, :].bitcast(U8)[:, cols],
+                    start=False,
+                    stop=(o == PASSES - 1),
+                )
 
         neg = held.tile([P, N], F32, name="neg")
         neg_max = [held.tile([P, 1], F32, name=f"neg_max{h}") for h in range(2)]

@@ -45,9 +45,9 @@ def tile_attend_residw_topk_kernel(tc, qT, k_words, k_scales, c_words, c_scales,
         def load_scales(tile, scales):
             nc.sync.dma_start(tile[0:P:4, :], scales.bitcast(I32).rearrange("o f t -> f o t"))
 
-        def move_scales(planes, got, first_row):
+        def move_scales(queue, planes, got, first_row):
             for quad in range(0, P, 32):
-                nc.scalar.dma_start(
+                queue.dma_start(
                     planes[quad + first_row : quad + first_row + 4, :, :], got[:].bitcast(I32)[quad : quad + 32 : 4, :]
                 )
 
@@ -71,11 +71,11 @@ def tile_attend_residw_topk_kernel(tc, qT, k_words, k_scales, c_words, c_scales,
 
         ks_got = held.tile([P, N], U8, name="ks_got", align_bytes=64)
         nc.vector.tensor_copy(ks_got[:], ks_all[:].bitcast(U8).indirect(offsets[:]))
-        move_scales(ks_planes, ks_got, 0)
+        move_scales(nc.scalar, ks_planes, ks_got, 0)
 
         cs_got = held.tile([P, N], U8, name="cs_got", align_bytes=64)
         nc.vector.tensor_copy(cs_got[:], cs_all[:].bitcast(U8).indirect(offsets[:]))
-        move_scales(cs_planes, cs_got, C_ROW)
+        move_scales(nc.sync, cs_planes, cs_got, C_ROW)
 
         q_codes = held.tile([P, PASSES * NQ], U32, name="q_codes", tag="cs_then_q", align_bytes=64)
         q_scales = held.tile([P, PASSES * NQ], U8, name="q_scales", align_bytes=64)

@@ -59,8 +59,7 @@ def tile_attend_residw_topk_kernel(tc, qT, k_words, k_scales, c_words, c_scales,
         load_scales(ks_all, k_scales)
         load_scales(cs_all, c_scales)
         nc.sync.dma_start(kw_all[:], k_words[0].rearrange("p t b -> p (t b)").bitcast(I32))
-        for o in range(PASSES):
-            nc.sync.dma_start(cw_all[o][:], c_words[o].rearrange("p t b -> p (t b)").bitcast(I32))
+        nc.sync.dma_start(cw_all[0][:], c_words[0].rearrange("p t b -> p (t b)").bitcast(I32))
 
         warm_out = held.tile([P, 8], F32, name="warm_out")
         nc.scalar.activation(warm_out[:], warm[:], ACT.Exp)
@@ -71,7 +70,8 @@ def tile_attend_residw_topk_kernel(tc, qT, k_words, k_scales, c_words, c_scales,
 
         ks_got = held.tile([P, N], U8, name="ks_got", align_bytes=64)
         nc.vector.tensor_copy(ks_got[:], ks_all[:].bitcast(U8).indirect(offsets[:]))
-        move_scales(nc.scalar, ks_planes, ks_got, 0)
+        move_scales(nc.sync, ks_planes, ks_got, 0)
+        nc.sync.dma_start(cw_all[1][:], c_words[1].rearrange("p t b -> p (t b)").bitcast(I32))
 
         cs_got = held.tile([P, N], U8, name="cs_got", align_bytes=64)
         nc.vector.tensor_copy(cs_got[:], cs_all[:].bitcast(U8).indirect(offsets[:]))

@@ -35,10 +35,8 @@ def tile_attend_residw_topk_kernel(tc, qT, k_words, k_scales, c_words, c_scales,
         cs_all = held.tile([P, T // 4], I32, name="cs_all", tag="cs_then_q", align_bytes=64)
         ks_planes = held.tile([P, PASSES, N // 4], I32, name="ks_planes", align_bytes=64)
         cs_planes = held.tile([P, PASSES, N // 4], I32, name="cs_planes", align_bytes=64)
-        warm = held.tile([P, 8], F32, name="warm")
         nc.vector.memset(ks_all[:], 0)
         nc.vector.memset(cs_all[:], 0)
-        nc.vector.memset(warm[:], 0.0)
         nc.vector.memset(ks_planes[:], 0)
         nc.vector.memset(cs_planes[:], 0)
 
@@ -60,9 +58,6 @@ def tile_attend_residw_topk_kernel(tc, qT, k_words, k_scales, c_words, c_scales,
         load_scales(cs_all, c_scales)
         nc.sync.dma_start(kw_all[:], k_words[0].rearrange("p t b -> p (t b)").bitcast(I32))
         nc.sync.dma_start(cw_all[0][:], c_words[0].rearrange("p t b -> p (t b)").bitcast(I32))
-
-        warm_out = held.tile([P, 8], F32, name="warm_out")
-        nc.scalar.activation(warm_out[:], warm[:], ACT.Exp)
 
         q_bf = held.tile([P, PASSES, NQ, PACK], BF16, name="q_bf", align_bytes=64)
         for o in range(PASSES):

@@ -32,7 +32,7 @@ def tile_attend_residw_topk_kernel(tc, qT, k_words, k_scales, c_words, c_scales,
 
         offsets = held.tile([P, N // 16], U16, name="offsets")
         ks_all = held.tile([P, T // 4], I32, name="ks_all", align_bytes=64)
-        cs_all = held.tile([P, T // 4], I32, name="cs_all", tag="cs_then_q", align_bytes=64)
+        cs_all = held.tile([P, T // 4], I32, name="cs_all", align_bytes=64)
         ks_planes = held.tile([P, PASSES, N // 4], I32, name="ks_planes", align_bytes=64)
         cs_planes = held.tile([P, PASSES, N // 4], I32, name="cs_planes", align_bytes=64)
         nc.vector.memset(ks_all[:], 0)
@@ -72,18 +72,20 @@ def tile_attend_residw_topk_kernel(tc, qT, k_words, k_scales, c_words, c_scales,
         nc.vector.tensor_copy(cs_got[:], cs_all[:].bitcast(U8).indirect(offsets[:]))
         move_scales(nc.sync, cs_planes, cs_got, C_ROW)
 
-        q_codes = held.tile([P, PASSES * NQ], U32, name="q_codes", tag="cs_then_q", align_bytes=64)
+        q_codes = held.tile([P, PASSES * NQ], U32, name="q_codes", align_bytes=64)
         q_scales = held.tile([P, PASSES * NQ], U8, name="q_scales", align_bytes=64)
         nc.vector.quantize_mx(
             out=q_codes[:].bitcast(FP8X4), scales=q_scales[:], in_=q_bf[:].rearrange("p o w j -> p (o w j)")
         )
 
-        kw_got = held.tile([P, N], U32, name="kw_got", align_bytes=64)
-        nc.vector.tensor_copy(kw_got[:], kw_all[:].bitcast(U32).indirect(offsets[:]))
-        kw_pass = held.tile([P, PASSES, N], U16, name="kw_pass", align_bytes=64)
-        kw_pairs = kw_got[:].bitcast(U16).rearrange("p (n o) -> p o n", o=PASSES)
-        for o in range(PASSES):
-            nc.vector.tensor_copy(kw_pass[:, o, :], kw_pairs[:, o, :])
+        kw_got = [held.tile([P, HALF], U32, name=f"kw_got{h}", align_bytes=64) for h in range(2)]
+        kw_pass = [held.tile([P, PASSES, HALF], U16, name=f"kw_pass{h}", align_bytes=64) for h in range(2)]
+        for h in range(2):
+            nc.vector.tensor_copy(
+                kw_got[h][:], kw_all[:].bitcast(U32).indirect(offsets[:, h * HALF // 16 : (h + 1) * HALF // 16])
+            )
+        for h in range(2):
+            nc.vector.tensor_copy(kw_pass[h][:], kw_got[h][:].bitcast(U16).rearrange("p (n o) -> p o n", o=PASSES))
 
         cw_got = [held.tile([P, N], U32, name=f"cw_got{o}", align_bytes=64) for o in range(PASSES)]
         nc.vector.tensor_copy(cw_got[0][:], cw_all[0][:].bitcast(U32).indirect(offsets[:]))
@@ -107,7 +109,7 @@ def tile_attend_residw_topk_kernel(tc, qT, k_words, k_scales, c_words, c_scales,
                     out=banks[h][:, c0 : c0 + QUART],
                     lhsT=lhsT,
                     lhsT_scale=lhsT_scale,
-                    rhs=kw_pass[:, o, n0 : n0 + QUART].bitcast(FP4X4),
+                    rhs=kw_pass[h][:, o, c0 : c0 + QUART].bitcast(FP4X4),
                     rhs_scale=ks_planes[:, o, :].bitcast(U8)[:, n0 : n0 + QUART],
                     start=(o == 0 and c0 == 0),
                     stop=False,

@@ -114,6 +114,18 @@ def tile_attend_residw_topk_kernel(tc, qT, k_words, k_scales, c_words, c_scales,
                     start=(o == 0 and c0 == 0),
                     stop=False,
                 )
+        warm = psum.tile([P, N], F32, name="warm")
+        lhsT, lhsT_scale = q_operand(PASSES - 1)
+        for h in range(2):
+            nc.tensor.matmul_mx(
+                out=warm[:, h * HALF : (h + 1) * HALF],
+                lhsT=lhsT,
+                lhsT_scale=lhsT_scale,
+                rhs=kw_pass[h][:, PASSES - 1, :].bitcast(FP4X4),
+                rhs_scale=ks_planes[:, PASSES - 1, :].bitcast(U8)[:, h * HALF : (h + 1) * HALF],
+                start=True,
+                stop=True,
+            )
         for o in range(PASSES):
             lhsT, lhsT_scale = q_operand(o)
             for h in range(2):

@@ -152,7 +152,5 @@ def tile_attend_residw_topk_kernel(tc, qT, k_words, k_scales, c_words, c_scales,
         inv = held.tile([P, 1], F32, name="inv")
         nc.vector.reciprocal(inv[:], total[:])
         y = held.tile([P, N], F32, name="y")
-        for h, queue in enumerate((nc.sync, nc.scalar)):
-            cols = slice(h * HALF, (h + 1) * HALF)
-            nc.vector.tensor_scalar(y[:, cols], e[:, cols], inv[:], None, ALU.mult)
-            queue.dma_start(out[0][:, cols], y[:, cols])
+        nc.vector.tensor_scalar(y[:], e[:], inv[:], None, ALU.mult)
+        nc.sync.dma_start(out[0], y[:])

@@ -114,18 +114,6 @@ def tile_attend_residw_topk_kernel(tc, qT, k_words, k_scales, c_words, c_scales,
                     start=(o == 0 and c0 == 0),
                     stop=False,
                 )
-        warm = psum.tile([P, N], F32, name="warm")
-        lhsT, lhsT_scale = q_operand(PASSES - 1)
-        for h in range(2):
-            nc.tensor.matmul_mx(
-                out=warm[:, h * HALF : (h + 1) * HALF],
-                lhsT=lhsT,
-                lhsT_scale=lhsT_scale,
-                rhs=kw_pass[h][:, PASSES - 1, :].bitcast(FP4X4),
-                rhs_scale=ks_planes[:, PASSES - 1, :].bitcast(U8)[:, h * HALF : (h + 1) * HALF],
-                start=True,
-                stop=True,
-            )
         for o in range(PASSES):
             lhsT, lhsT_scale = q_operand(o)
             for h in range(2):

@@ -114,10 +114,10 @@ def tile_attend_residw_topk_kernel(tc, qT, k_words, k_scales, c_words, c_scales,
                     start=(o == 0 and c0 == 0),
                     stop=False,
                 )
-        for o in range(PASSES):
-            lhsT, lhsT_scale = q_operand(o)
-            for h in range(2):
-                cols = slice(h * HALF, (h + 1) * HALF)
+        for h in range(2):
+            cols = slice(h * HALF, (h + 1) * HALF)
+            for o in range(PASSES):
+                lhsT, lhsT_scale = q_operand(o)
                 nc.tensor.matmul_mx(
                     out=banks[h][:],
                     lhsT=lhsT,

@@ -114,6 +114,17 @@ def tile_attend_residw_topk_kernel(tc, qT, k_words, k_scales, c_words, c_scales,
                     start=(o == 0 and c0 == 0),
                     stop=False,
                 )
+        warm = psum.tile([P, N], F32, name="warm")
+        lhsT, lhsT_scale = q_operand(PASSES - 1)
+        nc.tensor.matmul_mx(
+            out=warm[:],
+            lhsT=lhsT,
+            lhsT_scale=lhsT_scale,
+            rhs=kw_pass[1][:].rearrange("p o n -> p (o n)").bitcast(FP4X4),
+            rhs_scale=ks_planes[:, PASSES - 1, :].bitcast(U8),
+            start=True,
+            stop=True,
+        )
         for h in range(2):
             cols = slice(h * HALF, (h + 1) * HALF)
             for o in range(PASSES):

@@ -22,6 +22,7 @@ PASSES = D // (P * PACK)
 HALF = N // 2
 QUART = 128
 C_ROW = 4
+BURST = 256
 
 
 def tile_attend_residw_topk_kernel(tc, qT, k_words, k_scales, c_words, c_scales, offs, out):
@@ -30,11 +31,11 @@ def tile_attend_residw_topk_kernel(tc, qT, k_words, k_scales, c_words, c_scales,
         held = ctx.enter_context(tc.tile_pool(name="held", bufs=1))
         psum = ctx.enter_context(tc.psum_pool(name="psum", bufs=1))
 
-        offsets = held.tile([P, N // 16], U16, name="offsets")
-        ks_all = held.tile([P, T // 4], I32, name="ks_all", align_bytes=64)
-        cs_all = held.tile([P, T // 4], I32, name="cs_all", align_bytes=64)
-        ks_planes = held.tile([P, PASSES, N // 4], I32, name="ks_planes", align_bytes=64)
-        cs_planes = held.tile([P, PASSES, N // 4], I32, name="cs_planes", align_bytes=64)
+        offsets = held.tile([P, N // 16], U16, name="offsets", align_bytes=BURST)
+        ks_all = held.tile([P, T // 4], I32, name="ks_all", align_bytes=BURST)
+        cs_all = held.tile([P, T // 4], I32, name="cs_all", align_bytes=BURST)
+        ks_planes = held.tile([P, PASSES, N // 4], I32, name="ks_planes", align_bytes=BURST)
+        cs_planes = held.tile([P, PASSES, N // 4], I32, name="cs_planes", align_bytes=BURST)
         nc.vector.memset(ks_all[:], 0)
         nc.vector.memset(cs_all[:], 0)
         nc.vector.memset(ks_planes[:], 0)
@@ -49,9 +50,9 @@ def tile_attend_residw_topk_kernel(tc, qT, k_words, k_scales, c_words, c_scales,
                     planes[quad + first_row : quad + first_row + 4, :, :], got[:].bitcast(I32)[quad : quad + 32 : 4, :]
                 )
 
-        q_raw = held.tile([P, PASSES, PACK * NQ], F32, name="q_raw")
-        kw_all = held.tile([P, T], I32, name="kw_all", align_bytes=64)
-        cw_all = [held.tile([P, T], I32, name=f"cw_all{o}", align_bytes=64) for o in range(PASSES)]
+        q_raw = held.tile([P, PASSES, PACK * NQ], F32, name="q_raw", align_bytes=BURST)
+        kw_all = held.tile([P, T], I32, name="kw_all", align_bytes=BURST)
+        cw_all = [held.tile([P, T], I32, name=f"cw_all{o}", align_bytes=BURST) for o in range(PASSES)]
         nc.sync.dma_start(q_raw[:], qT[0].rearrange("(o p j) w -> p o (j w)", o=PASSES, j=PACK))
         nc.sync.dma_start(offsets[:], offs)
         load_scales(ks_all, k_scales)
@@ -63,12 +64,12 @@ def tile_attend_residw_topk_kernel(tc, qT, k_words, k_scales, c_words, c_scales,
         for o in range(PASSES):
             nc.scalar.copy(q_bf[:, o, :, :], q_raw[:, o, :].rearrange("p (j w) -> p w j", j=PACK))
 
-        ks_got = held.tile([P, N], U8, name="ks_got", align_bytes=64)
+        ks_got = held.tile([P, N], U8, name="ks_got", align_bytes=BURST)
         nc.vector.tensor_copy(ks_got[:], ks_all[:].bitcast(U8).indirect(offsets[:]))
         move_scales(nc.sync, ks_planes, ks_got, 0)
         nc.sync.dma_start(cw_all[1][:], c_words[1].rearrange("p t b -> p (t b)").bitcast(I32))
 
-        cs_got = held.tile([P, N], U8, name="cs_got", align_bytes=64)
+        cs_got = held.tile([P, N], U8, name="cs_got", align_bytes=BURST)
         nc.vector.tensor_copy(cs_got[:], cs_all[:].bitcast(U8).indirect(offsets[:]))
         move_scales(nc.sync, cs_planes, cs_got, C_ROW)
 
@@ -150,6 +151,6 @@ def tile_attend_residw_topk_kernel(tc, qT, k_words, k_scales, c_words, c_scales,
         nc.scalar.activation(e[:], neg[:], ACT.Exp, bias=neg_max[1][:], scale=-1.0, accum_out=total[:])
         inv = held.tile([P, 1], F32, name="inv")
         nc.vector.reciprocal(inv[:], total[:])
-        y = held.tile([P, N], F32, name="y")
+        y = held.tile([P, N], F32, name="y", align_bytes=BURST)
         nc.vector.tensor_scalar(y[:], e[:], inv[:], None, ALU.mult)
         nc.sync.dma_start(out[0], y[:])

@@ -90,11 +90,9 @@ def tile_attend_residw_topk_kernel(tc, qT, k_words, k_scales, c_words, c_scales,
 
         cw_got = [held.tile([P, N], U32, name=f"cw_got{o}", align_bytes=64) for o in range(PASSES)]
         nc.vector.tensor_copy(cw_got[0][:], cw_all[0][:].bitcast(U32).indirect(offsets[:]))
-        for h in range(2):
-            nc.vector.tensor_copy(
-                cw_got[1][:, h * HALF : (h + 1) * HALF],
-                cw_all[1][:].bitcast(U32).indirect(offsets[:, h * HALF // 16 : (h + 1) * HALF // 16]),
-            )
+        last_cuts = [(a, a + QUART) for a in range(0, N, QUART)]
+        for a, b in last_cuts:
+            nc.vector.tensor_copy(cw_got[1][:, a:b], cw_all[1][:].bitcast(U32).indirect(offsets[:, a // 16 : b // 16]))
 
         banks = [psum.tile([P, HALF], F32, name=f"bank{h}") for h in range(2)]
 
@@ -115,30 +113,21 @@ def tile_attend_residw_topk_kernel(tc, qT, k_words, k_scales, c_words, c_scales,
                     start=(o == 0 and c0 == 0),
                     stop=False,
                 )
-        warm = psum.tile([P, N], F32, name="warm")
-        lhsT, lhsT_scale = q_operand(PASSES - 1)
-        nc.tensor.matmul_mx(
-            out=warm[:],
-            lhsT=lhsT,
-            lhsT_scale=lhsT_scale,
-            rhs=kw_pass[1][:].rearrange("p o n -> p (o n)").bitcast(FP4X4),
-            rhs_scale=ks_planes[:, PASSES - 1, :].bitcast(U8),
-            start=True,
-            stop=True,
-        )
-        for h in range(2):
-            cols = slice(h * HALF, (h + 1) * HALF)
-            for o in range(PASSES):
-                lhsT, lhsT_scale = q_operand(o)
-                nc.tensor.matmul_mx(
-                    out=banks[h][:],
-                    lhsT=lhsT,
-                    lhsT_scale=lhsT_scale,
-                    rhs=cw_got[o][:, cols].bitcast(FP8X4),
-                    rhs_scale=cs_planes[C_ROW:P, o, :].bitcast(U8)[:, cols],
-                    start=False,
-                    stop=(o == PASSES - 1),
-                )
+        fine = []
+        for first in (0, HALF):
+            fine.extend([(0, first, first + HALF), (1, first, first + QUART), (1, first + QUART, first + HALF)])
+        for o, a, b in fine:
+            h = a // HALF
+            lhsT, lhsT_scale = q_operand(o)
+            nc.tensor.matmul_mx(
+                out=banks[h][:, a - h * HALF : b - h * HALF],
+                lhsT=lhsT,
+                lhsT_scale=lhsT_scale,
+                rhs=cw_got[o][:, a:b].bitcast(FP8X4),
+                rhs_scale=cs_planes[C_ROW:P, o, :].bitcast(U8)[:, a:b],
+                start=False,
+                stop=(o == PASSES - 1 and b % HALF == 0),
+            )
 
         neg = held.tile([P, N], F32, name="neg")
         neg_max = [held.tile([P, 1], F32, name=f"neg_max{h}") for h in range(2)]

@@ -41,8 +41,6 @@ def tile_attend_residw_topk_kernel(tc, qT, k_words, k_scales, c_words, c_scales,
         nc.vector.memset(ks_planes[:], 0)
         nc.vector.memset(cs_planes[:], 0)
 
-        def load_scales(tile, scales):
-            nc.sync.dma_start(tile[0:P:4, :], scales.bitcast(I32).rearrange("o f t -> f o t"))
 
         def move_scales(queue, planes, got, first_row):
             for quad in range(0, P, 32):
@@ -55,8 +53,8 @@ def tile_attend_residw_topk_kernel(tc, qT, k_words, k_scales, c_words, c_scales,
         cw_all = [held.tile([P, T], I32, name=f"cw_all{o}", align_bytes=BURST) for o in range(PASSES)]
         nc.sync.dma_start(q_raw[:], qT[0].rearrange("(o p j) w -> p o (j w)", o=PASSES, j=PACK))
         nc.sync.dma_start(offsets[:], offs)
-        load_scales(ks_all, k_scales)
-        load_scales(cs_all, c_scales)
+        nc.sync.dma_start(ks_all[0:P:4, :], k_scales.bitcast(I32).rearrange("o f t -> f o t"))
+        nc.sync.dma_start(cs_all[0:P:4, :], c_scales.bitcast(I32).rearrange("o f t -> (o f) t"))
         nc.sync.dma_start(kw_all[:], k_words[0].rearrange("p t b -> p (t b)").bitcast(I32))
         nc.sync.dma_start(cw_all[0][:], c_words[0].rearrange("p t b -> p (t b)").bitcast(I32))
 
@@ -71,7 +69,14 @@ def tile_attend_residw_topk_kernel(tc, qT, k_words, k_scales, c_words, c_scales,
 
         cs_got = held.tile([P, N], U8, name="cs_got", align_bytes=BURST)
         nc.vector.tensor_copy(cs_got[:], cs_all[:].bitcast(U8).indirect(offsets[:]))
-        move_scales(nc.sync, cs_planes, cs_got, C_ROW)
+        cs_staged = held.tile([P, PASSES, N // 4], I32, name="cs_staged", align_bytes=BURST)
+        for o in range(PASSES):
+            nc.vector.tensor_copy(cs_staged[0:64, o, :], cs_got[:].bitcast(I32)[64 * o : 64 * (o + 1), :])
+        for r in range(4):
+            nc.sync.dma_start(
+                cs_planes[C_ROW + r : P : 32].rearrange("p o n -> p (o n)"),
+                cs_staged[4 * r : 64 : 16].rearrange("p o n -> p (o n)"),
+            )
 
         q_codes = held.tile([P, PASSES * NQ], U32, name="q_codes", align_bytes=64)
         q_scales = held.tile([P, PASSES * NQ], U8, name="q_scales", align_bytes=64)

from contextlib import ExitStack

import concourse.mybir as mybir

N, T, D, NQ = 512, 2048, 1024, 128
FLOPS = 2 * 2 * NQ * N * D

F32 = mybir.dt.float32
BF16 = mybir.dt.bfloat16
I32 = mybir.dt.int32
U32 = mybir.dt.uint32
U16 = mybir.dt.uint16
U8 = mybir.dt.uint8
FP8X4 = mybir.dt.float8_e4m3fn_x4
FP4X4 = mybir.dt.float4_e2m1fn_x4
ALU = mybir.AluOpType
ACT = mybir.ActivationFunctionType

P = 128
PACK = 4
PASSES = D // (P * PACK)
HALF = N // 2
QUART = 128
C_ROW = 4
BURST = 256


def tile_attend_residw_topk_kernel(tc, qT, k_words, k_scales, c_words, c_scales, offs, out):
    nc = tc.nc
    with ExitStack() as ctx:
        held = ctx.enter_context(tc.tile_pool(name="held", bufs=1))
        psum = ctx.enter_context(tc.psum_pool(name="psum", bufs=1))

        offsets = held.tile([P, N // 16], U16, name="offsets", align_bytes=BURST)
        ks_all = held.tile([P, T // 4], I32, name="ks_all", align_bytes=BURST)
        cs_all = held.tile([P, T // 4], I32, name="cs_all", align_bytes=BURST)
        ks_planes = held.tile([P, PASSES, N // 4], I32, name="ks_planes", align_bytes=BURST)
        cs_planes = held.tile([P, PASSES, N // 4], I32, name="cs_planes", align_bytes=BURST)
        nc.vector.memset(ks_all[:], 0)
        nc.vector.memset(cs_all[:], 0)
        nc.vector.memset(ks_planes[:], 0)
        nc.vector.memset(cs_planes[:], 0)


        def move_scales(queue, planes, got, first_row):
            for quad in range(0, P, 32):
                queue.dma_start(
                    planes[quad + first_row : quad + first_row + 4, :, :], got[:].bitcast(I32)[quad : quad + 32 : 4, :]
                )

        q_raw = held.tile([P, PASSES, PACK * NQ], F32, name="q_raw", align_bytes=BURST)
        kw_all = held.tile([P, T], I32, name="kw_all", align_bytes=BURST)
        cw_all = [held.tile([P, T], I32, name=f"cw_all{o}", align_bytes=BURST) for o in range(PASSES)]
        nc.sync.dma_start(q_raw[:], qT[0].rearrange("(o p j) w -> p o (j w)", o=PASSES, j=PACK))
        nc.sync.dma_start(offsets[:], offs)
        nc.sync.dma_start(ks_all[0:P:4, :], k_scales.bitcast(I32).rearrange("o f t -> f o t"))
        nc.sync.dma_start(cs_all[0:P:4, :], c_scales.bitcast(I32).rearrange("o f t -> (o f) t"))
        nc.sync.dma_start(kw_all[:], k_words[0].rearrange("p t b -> p (t b)").bitcast(I32))
        nc.sync.dma_start(cw_all[0][:], c_words[0].rearrange("p t b -> p (t b)").bitcast(I32))

        q_bf = held.tile([P, PASSES, NQ, PACK], BF16, name="q_bf", align_bytes=64)
        for o in range(PASSES):
            nc.scalar.copy(q_bf[:, o, :, :], q_raw[:, o, :].rearrange("p (j w) -> p w j", j=PACK))

        ks_got = held.tile([P, N], U8, name="ks_got", align_bytes=BURST)
        nc.vector.tensor_copy(ks_got[:], ks_all[:].bitcast(U8).indirect(offsets[:]))
        move_scales(nc.sync, ks_planes, ks_got, 0)
        nc.sync.dma_start(cw_all[1][:], c_words[1].rearrange("p t b -> p (t b)").bitcast(I32))

        cs_got = held.tile([P, N], U8, name="cs_got", align_bytes=BURST)
        nc.vector.tensor_copy(cs_got[:], cs_all[:].bitcast(U8).indirect(offsets[:]))
        cs_staged = held.tile([P, PASSES, N // 4], I32, name="cs_staged", align_bytes=BURST)
        for o in range(PASSES):
            nc.vector.tensor_copy(cs_staged[0:64, o, :], cs_got[:].bitcast(I32)[64 * o : 64 * (o + 1), :])
        for r in range(4):
            nc.sync.dma_start(
                cs_planes[C_ROW + r : P : 32].rearrange("p o n -> p (o n)"),
                cs_staged[4 * r : 64 : 16].rearrange("p o n -> p (o n)"),
            )

        q_codes = held.tile([P, PASSES * NQ], U32, name="q_codes", align_bytes=64)
        q_scales = held.tile([P, PASSES * NQ], U8, name="q_scales", align_bytes=64)
        nc.vector.quantize_mx(
            out=q_codes[:].bitcast(FP8X4), scales=q_scales[:], in_=q_bf[:].rearrange("p o w j -> p (o w j)")
        )

        kw_got = [held.tile([P, HALF], U32, name=f"kw_got{h}", align_bytes=64) for h in range(2)]
        kw_pass = [held.tile([P, PASSES, HALF], U16, name=f"kw_pass{h}", align_bytes=64) for h in range(2)]
        for h in range(2):
            nc.vector.tensor_copy(
                kw_got[h][:], kw_all[:].bitcast(U32).indirect(offsets[:, h * HALF // 16 : (h + 1) * HALF // 16])
            )
        for h in range(2):
            nc.vector.tensor_copy(kw_pass[h][:], kw_got[h][:].bitcast(U16).rearrange("p (n o) -> p o n", o=PASSES))

        cw_got = [held.tile([P, N], U32, name=f"cw_got{o}", align_bytes=64) for o in range(PASSES)]
        nc.vector.tensor_copy(cw_got[0][:], cw_all[0][:].bitcast(U32).indirect(offsets[:]))
        last_cuts = [(a, a + QUART) for a in range(0, N, QUART)]
        for a, b in last_cuts:
            nc.vector.tensor_copy(cw_got[1][:, a:b], cw_all[1][:].bitcast(U32).indirect(offsets[:, a // 16 : b // 16]))

        banks = [psum.tile([P, HALF], F32, name=f"bank{h}") for h in range(2)]

        def q_operand(o):
            cols = slice(o * NQ, (o + 1) * NQ)
            return q_codes[:, cols].bitcast(FP8X4), q_scales[:, cols]

        for o in range(PASSES):
            lhsT, lhsT_scale = q_operand(o)
            for n0 in range(0, N, QUART):
                h, c0 = divmod(n0, HALF)
                nc.tensor.matmul_mx(
                    out=banks[h][:, c0 : c0 + QUART],
                    lhsT=lhsT,
                    lhsT_scale=lhsT_scale,
                    rhs=kw_pass[h][:, o, c0 : c0 + QUART].bitcast(FP4X4),
                    rhs_scale=ks_planes[:, o, :].bitcast(U8)[:, n0 : n0 + QUART],
                    start=(o == 0 and c0 == 0),
                    stop=False,
                )
        fine = []
        for first in (0, HALF):
            fine.extend([(0, first, first + HALF), (1, first, first + QUART), (1, first + QUART, first + HALF)])
        for o, a, b in fine:
            h = a // HALF
            lhsT, lhsT_scale = q_operand(o)
            nc.tensor.matmul_mx(
                out=banks[h][:, a - h * HALF : b - h * HALF],
                lhsT=lhsT,
                lhsT_scale=lhsT_scale,
                rhs=cw_got[o][:, a:b].bitcast(FP8X4),
                rhs_scale=cs_planes[C_ROW:P, o, :].bitcast(U8)[:, a:b],
                start=False,
                stop=(o == PASSES - 1 and b % HALF == 0),
            )

        neg = held.tile([P, N], F32, name="neg")
        neg_max = [held.tile([P, 1], F32, name=f"neg_max{h}") for h in range(2)]
        nc.vector.tensor_scalar(neg[:, 0:HALF], banks[0][:], -1.0, None, ALU.mult, ALU.min, accum_out=neg_max[0][:])
        nc.vector.tensor_scalar(
            neg[:, HALF:N], banks[1][:], -1.0, neg_max[0][:], ALU.mult, ALU.min, accum_out=neg_max[1][:]
        )
        e = held.tile([P, N], F32, name="e")
        total = held.tile([P, 1], F32, name="total")
        nc.scalar.activation(e[:], neg[:], ACT.Exp, bias=neg_max[1][:], scale=-1.0, accum_out=total[:])
        inv = held.tile([P, 1], F32, name="inv")
        nc.vector.reciprocal(inv[:], total[:])
        y = held.tile([P, N], F32, name="y", align_bytes=BURST)
        nc.vector.tensor_scalar(y[:], e[:], inv[:], None, ALU.mult)
        nc.sync.dma_start(out[0], y[:])
